import numpy as np
CORES = [0,1,2,3,4,5,6,7,8,9,10,11,12,13,14,15]
N = 16
def setup_inputs(rng):
    return {"x1": rng.standard_normal((N, 128, 1024), dtype=np.float32), "x2": rng.standard_normal((N, 128, 4), dtype=np.float32), "x3": rng.standard_normal((N, 128, 256), dtype=np.float32)}
def reference(x1, x2, x3):
    out = {}
    s = x1.sum(axis=0, dtype=np.float64).astype(x1.dtype)
    out["y1"] = np.broadcast_to(s, (N,) + s.shape)
    s = x2.sum(axis=0, dtype=np.float64).astype(x2.dtype)
    out["y2"] = np.broadcast_to(s, (N,) + s.shape)
    s = x3.sum(axis=0, dtype=np.float64).astype(x3.dtype)
    out["y3"] = np.broadcast_to(s, (N,) + s.shape)
    return out

@@ -1,0 +1,75 @@
+from concourse.bass import RemoteDMATransfer, DstId
+from concourse.mybir import AluOpType
+
+W = 1284
+S = 321
+GATE = [2, 3, 6, 7]
+FIN = [0, 1, 4, 5]
+
+SCRATCH = {
+    "buf": ("sbuf", [128, W], "float32"),
+    "land": ("sbuf", [128, 7 * S], "float32"),
+    "peer": ("sbuf", [128, S], "float32"),
+    "res": ("sbuf", [128, W], "float32"),
+}
+SEMAPHORES = ["loaded", "read1", "read2", "read3", "arr1", "arr2", "arr3", "acc", "stored"]
+
+
+def rank_program(g, core, T, topo):
+    if T.rank_of(core) is None:
+        return
+    base = 8 * topo.chip(core)
+    other = 8 * (topo.chip(core) ^ 1)
+    k = core - base
+
+    def dst(c):
+        rid, pid, se = topo.addr(c)
+        return DstId(rid=rid, pnc=pid)
+
+    def sh(t, s):
+        return t[:, s * S:(s + 1) * S]
+
+    g.dma_start(T.buf[:, 0:1024], T.x1[:, :]).then_inc(T.sem.loaded, 16)
+    g.dma_start(T.buf[:, 1024:1280], T.x3[:, :]).then_inc(T.sem.loaded, 16)
+    g.dma_start(T.buf[:, 1280:1284], T.x2[:, :]).then_inc(T.sem.loaded, 16)
+    g.wait_ge(T.sem.loaded, 48)
+
+    trs = []
+    for s, gk in enumerate(GATE):
+        if gk == k:
+            continue
+        slot = k if k < gk else k - 1
+        trs.append(RemoteDMATransfer(dst_ids=[dst(base + gk)], dma_engine_mask=0xF << (4 * s), remote_sem=T.sem.arr1,
+                                     src=sh(T.buf, s), dst=sh(T.land, slot)))
+    g.remote_dma_fused(trs, local_sem=T.sem.read1)
+
+    if k in GATE:
+        s = GATE.index(k)
+        g.wait_ge(T.sem.arr1, 28)
+        g.remote_dma_fused([RemoteDMATransfer(
+            dst_ids=[dst(base + FIN[s]), dst(other + FIN[s])], dma_engine_mask=0x00FF, remote_sem=T.sem.arr2,
+            srcs=[sh(T.buf, s)] + [sh(T.land, j) for j in range(7)], dsts=[sh(T.res, s), T.peer[:, :]], alu_op=1)],
+            local_sem=T.sem.read2)
+
+    if k in FIN:
+        s = FIN.index(k)
+        g.wait_ge(T.sem.arr2, 16)
+        peers = [base + j for j in range(8) if j != k]
+        g.remote_dma_fused([RemoteDMATransfer(
+            dst_ids=[dst(c) for c in peers], dma_engine_mask=0xFFFF, remote_sem=T.sem.arr3,
+            srcs=[sh(T.res, s), T.peer[:, :]], dsts=[sh(T.res, s) for c in peers], alu_op=1)],
+            local_sem=T.sem.read3)
+        g.wait_ge(T.sem.read3, 16)
+        g.dma_start(sh(T.res, s), T.peer[:, :], accum_op=AluOpType.add).then_inc(T.sem.acc, 16)
+        g.wait_ge(T.sem.acc, 16)
+        g.wait_ge(T.sem.arr3, 48)
+    else:
+        g.wait_ge(T.sem.arr3, 64)
+
+    g.dma_start(T.y1[:, :], T.res[:, 0:1024]).then_inc(T.sem.stored, 16)
+    g.dma_start(T.y3[:, :], T.res[:, 1024:1280]).then_inc(T.sem.stored, 16)
+    g.dma_start(T.y2[:, :], T.res[:, 1280:1284]).then_inc(T.sem.stored, 16)
+    g.wait_ge(T.sem.read1, 4 * len(trs))
+    if k in GATE:
+        g.wait_ge(T.sem.read2, 8)
+    g.wait_ge(T.sem.stored, 48)

@@ -1,15 +1,17 @@
 from concourse.bass import RemoteDMATransfer, DstId
 from concourse.mybir import AluOpType
 
-W = 1284
-S = 321
+W = 1288
+S = 322
+P = 161
 GATE = [2, 3, 6, 7]
-FIN = [0, 1, 4, 5]
+FIN = [0, 3, 1, 2, 4, 7, 5, 6]
 
 SCRATCH = {
     "buf": ("sbuf", [128, W], "float32"),
     "land": ("sbuf", [128, 7 * S], "float32"),
-    "peer": ("sbuf", [128, S], "float32"),
+    "mine": ("sbuf", [128, P], "float32"),
+    "peer": ("sbuf", [128, P], "float32"),
     "res": ("sbuf", [128, W], "float32"),
 }
 SEMAPHORES = ["loaded", "read1", "read2", "read3", "arr1", "arr2", "arr3", "acc", "stored"]
@@ -29,10 +31,14 @@ def rank_program(g, core, T, topo):
     def sh(t, s):
         return t[:, s * S:(s + 1) * S]
 
+    def pc(t, p):
+        return t[:, p * P:(p + 1) * P]
+
     g.dma_start(T.buf[:, 0:1024], T.x1[:, :]).then_inc(T.sem.loaded, 16)
     g.dma_start(T.buf[:, 1024:1280], T.x3[:, :]).then_inc(T.sem.loaded, 16)
     g.dma_start(T.buf[:, 1280:1284], T.x2[:, :]).then_inc(T.sem.loaded, 16)
-    g.wait_ge(T.sem.loaded, 48)
+    g.dma_start(T.buf[:, 1284:1288], T.x2[:, :]).then_inc(T.sem.loaded, 16)
+    g.wait_ge(T.sem.loaded, 64)
 
     trs = []
     for s, gk in enumerate(GATE):
@@ -46,30 +52,33 @@ def rank_program(g, core, T, topo):
     if k in GATE:
         s = GATE.index(k)
         g.wait_ge(T.sem.arr1, 28)
-        g.remote_dma_fused([RemoteDMATransfer(
-            dst_ids=[dst(base + FIN[s]), dst(other + FIN[s])], dma_engine_mask=0x00FF, remote_sem=T.sem.arr2,
-            srcs=[sh(T.buf, s)] + [sh(T.land, j) for j in range(7)], dsts=[sh(T.res, s), T.peer[:, :]], alu_op=1)],
-            local_sem=T.sem.read2)
+        t2 = []
+        for h in range(2):
+            p = 2 * s + h
+            srcs = [pc(T.buf, p)] + [pc(T.land, 2 * j + h) for j in range(7)]
+            t2.append(RemoteDMATransfer(dst_ids=[dst(other + FIN[p])], dma_engine_mask=0xF << (4 * h),
+                                        remote_sem=T.sem.arr2, srcs=srcs, dsts=[T.peer[:, :]], alu_op=1))
+            t2.append(RemoteDMATransfer(dst_ids=[dst(base + FIN[p]), dst(base + FIN[p])],
+                                        dma_engine_mask=0xF << (8 + 4 * h), remote_sem=T.sem.arr2, srcs=srcs,
+                                        dsts=[T.mine[:, :], pc(T.res, p)], alu_op=1))
+        g.remote_dma_fused(t2, local_sem=T.sem.read2)
 
-    if k in FIN:
-        s = FIN.index(k)
-        g.wait_ge(T.sem.arr2, 16)
-        peers = [base + j for j in range(8) if j != k]
-        g.remote_dma_fused([RemoteDMATransfer(
-            dst_ids=[dst(c) for c in peers], dma_engine_mask=0xFFFF, remote_sem=T.sem.arr3,
-            srcs=[sh(T.res, s), T.peer[:, :]], dsts=[sh(T.res, s) for c in peers], alu_op=1)],
-            local_sem=T.sem.read3)
-        g.wait_ge(T.sem.read3, 16)
-        g.dma_start(sh(T.res, s), T.peer[:, :], accum_op=AluOpType.add).then_inc(T.sem.acc, 16)
-        g.wait_ge(T.sem.acc, 16)
-        g.wait_ge(T.sem.arr3, 48)
-    else:
-        g.wait_ge(T.sem.arr3, 64)
+    p = FIN.index(k)
+    g.wait_ge(T.sem.arr2, 12)
+    peers = [base + j for j in range(8) if j != k]
+    g.remote_dma_fused([RemoteDMATransfer(
+        dst_ids=[dst(c) for c in peers], dma_engine_mask=0xFFFF, remote_sem=T.sem.arr3,
+        srcs=[T.mine[:, :], T.peer[:, :]], dsts=[pc(T.res, p) for c in peers], alu_op=1)],
+        local_sem=T.sem.read3)
+    g.dma_start(pc(T.res, p), T.peer[:, :], accum_op=AluOpType.add).then_inc(T.sem.acc, 16)
+    g.wait_ge(T.sem.acc, 16)
+    g.wait_ge(T.sem.arr3, 112)
 
     g.dma_start(T.y1[:, :], T.res[:, 0:1024]).then_inc(T.sem.stored, 16)
     g.dma_start(T.y3[:, :], T.res[:, 1024:1280]).then_inc(T.sem.stored, 16)
     g.dma_start(T.y2[:, :], T.res[:, 1280:1284]).then_inc(T.sem.stored, 16)
     g.wait_ge(T.sem.read1, 4 * len(trs))
     if k in GATE:
-        g.wait_ge(T.sem.read2, 8)
+        g.wait_ge(T.sem.read2, 16)
+    g.wait_ge(T.sem.read3, 16)
     g.wait_ge(T.sem.stored, 48)

@@ -2,19 +2,19 @@ from concourse.bass import RemoteDMATransfer, DstId
 from concourse.mybir import AluOpType
 
 W = 1288
-S = 322
+C = 644
 P = 161
 GATE = [2, 3, 6, 7]
-FIN = [0, 3, 1, 2, 4, 7, 5, 6]
+FIN = [0, 1, 4, 5, 3, 2, 7, 6]
 
 SCRATCH = {
     "buf": ("sbuf", [128, W], "float32"),
-    "land": ("sbuf", [128, 7 * S], "float32"),
+    "land": ("sbuf", [128, 14 * P], "float32"),
     "mine": ("sbuf", [128, P], "float32"),
     "peer": ("sbuf", [128, P], "float32"),
     "res": ("sbuf", [128, W], "float32"),
 }
-SEMAPHORES = ["loaded", "read1", "read2", "read3", "arr1", "arr2", "arr3", "acc", "stored"]
+SEMAPHORES = ["load0", "load1", "read1", "read2", "read3", "arr1a", "arr1b", "arr2", "arr3a", "arr3b", "acc", "stored"]
 
 
 def rank_program(g, core, T, topo):
@@ -23,62 +23,70 @@ def rank_program(g, core, T, topo):
     base = 8 * topo.chip(core)
     other = 8 * (topo.chip(core) ^ 1)
     k = core - base
+    gate = k in GATE
+    arr1 = [T.sem.arr1a, T.sem.arr1b]
+    arr3 = [T.sem.arr3a, T.sem.arr3b]
 
     def dst(c):
         rid, pid, se = topo.addr(c)
         return DstId(rid=rid, pnc=pid)
 
-    def sh(t, s):
-        return t[:, s * S:(s + 1) * S]
+    def pc(t, q):
+        return t[:, q * P:(q + 1) * P]
 
-    def pc(t, p):
-        return t[:, p * P:(p + 1) * P]
+    g.dma_start(T.buf[:, 0:C], T.x1[:, 0:C]).then_inc(T.sem.load0, 16)
+    g.dma_start(T.buf[:, C:1024], T.x1[:, C:1024]).then_inc(T.sem.load1, 16)
+    g.dma_start(T.buf[:, 1024:1280], T.x3[:, :]).then_inc(T.sem.load1, 16)
+    g.dma_start(T.buf[:, 1280:1284], T.x2[:, :]).then_inc(T.sem.load1, 16)
+    g.dma_start(T.buf[:, 1284:1288], T.x2[:, :]).then_inc(T.sem.load1, 16)
 
-    g.dma_start(T.buf[:, 0:1024], T.x1[:, :]).then_inc(T.sem.loaded, 16)
-    g.dma_start(T.buf[:, 1024:1280], T.x3[:, :]).then_inc(T.sem.loaded, 16)
-    g.dma_start(T.buf[:, 1280:1284], T.x2[:, :]).then_inc(T.sem.loaded, 16)
-    g.dma_start(T.buf[:, 1284:1288], T.x2[:, :]).then_inc(T.sem.loaded, 16)
-    g.wait_ge(T.sem.loaded, 64)
+    n1 = 0
+    for c in range(2):
+        g.wait_ge([T.sem.load0, T.sem.load1][c], [16, 64][c])
+        trs = []
+        for s, gk in enumerate(GATE):
+            if gk == k:
+                continue
+            slot = k if k < gk else k - 1
+            trs.append(RemoteDMATransfer(dst_ids=[dst(base + gk)], dma_engine_mask=0xF << (4 * s), remote_sem=arr1[c],
+                                         src=pc(T.buf, 4 * c + s), dst=pc(T.land, 7 * c + slot)))
+        g.remote_dma_fused(trs, local_sem=T.sem.read1)
+        n1 += 4 * len(trs)
 
-    trs = []
-    for s, gk in enumerate(GATE):
-        if gk == k:
-            continue
-        slot = k if k < gk else k - 1
-        trs.append(RemoteDMATransfer(dst_ids=[dst(base + gk)], dma_engine_mask=0xF << (4 * s), remote_sem=T.sem.arr1,
-                                     src=sh(T.buf, s), dst=sh(T.land, slot)))
-    g.remote_dma_fused(trs, local_sem=T.sem.read1)
-
-    if k in GATE:
+    if gate:
         s = GATE.index(k)
-        g.wait_ge(T.sem.arr1, 28)
-        t2 = []
-        for h in range(2):
-            p = 2 * s + h
-            srcs = [pc(T.buf, p)] + [pc(T.land, 2 * j + h) for j in range(7)]
-            t2.append(RemoteDMATransfer(dst_ids=[dst(other + FIN[p])], dma_engine_mask=0xF << (4 * h),
-                                        remote_sem=T.sem.arr2, srcs=srcs, dsts=[T.peer[:, :]], alu_op=1))
-            t2.append(RemoteDMATransfer(dst_ids=[dst(base + FIN[p]), dst(base + FIN[p])],
-                                        dma_engine_mask=0xF << (8 + 4 * h), remote_sem=T.sem.arr2, srcs=srcs,
-                                        dsts=[T.mine[:, :], pc(T.res, p)], alu_op=1))
-        g.remote_dma_fused(t2, local_sem=T.sem.read2)
+        for c in range(2):
+            q = 4 * c + s
+            g.wait_ge(arr1[c], 28)
+            srcs = [pc(T.buf, q)] + [pc(T.land, 7 * c + j) for j in range(7)]
+            g.remote_dma_fused([
+                RemoteDMATransfer(dst_ids=[dst(other + FIN[q])], dma_engine_mask=0x00FF,
+                                  remote_sem=T.sem.arr2, srcs=srcs, dsts=[T.peer[:, :]], alu_op=1),
+                RemoteDMATransfer(dst_ids=[dst(base + FIN[q]), dst(base + FIN[q])], dma_engine_mask=0xFF00,
+                                  remote_sem=T.sem.arr2, srcs=srcs, dsts=[T.mine[:, :], pc(T.res, q)], alu_op=1)],
+                local_sem=T.sem.read2)
 
-    p = FIN.index(k)
-    g.wait_ge(T.sem.arr2, 12)
+    q = FIN.index(k)
+    g.wait_ge(T.sem.arr2, 24)
     peers = [base + j for j in range(8) if j != k]
     g.remote_dma_fused([RemoteDMATransfer(
-        dst_ids=[dst(c) for c in peers], dma_engine_mask=0xFFFF, remote_sem=T.sem.arr3,
-        srcs=[T.mine[:, :], T.peer[:, :]], dsts=[pc(T.res, p) for c in peers], alu_op=1)],
+        dst_ids=[dst(c) for c in peers], dma_engine_mask=0xFFFF, remote_sem=arr3[q // 4],
+        srcs=[T.mine[:, :], T.peer[:, :]], dsts=[pc(T.res, q) for c in peers], alu_op=1)],
         local_sem=T.sem.read3)
-    g.dma_start(pc(T.res, p), T.peer[:, :], accum_op=AluOpType.add).then_inc(T.sem.acc, 16)
-    g.wait_ge(T.sem.acc, 16)
-    g.wait_ge(T.sem.arr3, 112)
+    g.dma_start(pc(T.res, q), T.peer[:, :], accum_op=AluOpType.add).then_inc(T.sem.acc, 16)
 
-    g.dma_start(T.y1[:, :], T.res[:, 0:1024]).then_inc(T.sem.stored, 16)
+    if not gate:
+        g.wait_ge(T.sem.acc, 16)
+    g.wait_ge(T.sem.arr3a, 64 if gate else 48)
+    g.dma_start(T.y1[:, 0:C], T.res[:, 0:C]).then_inc(T.sem.stored, 16)
+    if gate:
+        g.wait_ge(T.sem.acc, 16)
+    g.wait_ge(T.sem.arr3b, 48 if gate else 64)
+    g.dma_start(T.y1[:, C:1024], T.res[:, C:1024]).then_inc(T.sem.stored, 16)
     g.dma_start(T.y3[:, :], T.res[:, 1024:1280]).then_inc(T.sem.stored, 16)
     g.dma_start(T.y2[:, :], T.res[:, 1280:1284]).then_inc(T.sem.stored, 16)
-    g.wait_ge(T.sem.read1, 4 * len(trs))
-    if k in GATE:
-        g.wait_ge(T.sem.read2, 16)
+    g.wait_ge(T.sem.read1, n1)
+    if gate:
+        g.wait_ge(T.sem.read2, 32)
     g.wait_ge(T.sem.read3, 16)
-    g.wait_ge(T.sem.stored, 48)
+    g.wait_ge(T.sem.stored, 64)

@@ -5,16 +5,17 @@ W = 1288
 C = 644
 P = 161
 GATE = [2, 3, 6, 7]
-FIN = [0, 1, 4, 5, 3, 2, 7, 6]
+FIN = [0, 1, 4, 5]
 
 SCRATCH = {
     "buf": ("sbuf", [128, W], "float32"),
     "land": ("sbuf", [128, 14 * P], "float32"),
-    "mine": ("sbuf", [128, P], "float32"),
-    "peer": ("sbuf", [128, P], "float32"),
+    "mine": ("sbuf", [128, 2 * P], "float32"),
+    "peer": ("sbuf", [128, 2 * P], "float32"),
     "res": ("sbuf", [128, W], "float32"),
 }
-SEMAPHORES = ["load0", "load1", "read1", "read2", "read3", "arr1a", "arr1b", "arr2", "arr3a", "arr3b", "acc", "stored"]
+SEMAPHORES = ["load0", "load1", "read1", "read2", "read3", "arr1a", "arr1b", "arr2a", "arr2b", "arr3a", "arr3b",
+              "acc0", "acc1", "stored"]
 
 
 def rank_program(g, core, T, topo):
@@ -25,7 +26,9 @@ def rank_program(g, core, T, topo):
     k = core - base
     gate = k in GATE
     arr1 = [T.sem.arr1a, T.sem.arr1b]
+    arr2 = [T.sem.arr2a, T.sem.arr2b]
     arr3 = [T.sem.arr3a, T.sem.arr3b]
+    acc = [T.sem.acc0, T.sem.acc1]
 
     def dst(c):
         rid, pid, se = topo.addr(c)
@@ -60,33 +63,36 @@ def rank_program(g, core, T, topo):
             g.wait_ge(arr1[c], 28)
             srcs = [pc(T.buf, q)] + [pc(T.land, 7 * c + j) for j in range(7)]
             g.remote_dma_fused([
-                RemoteDMATransfer(dst_ids=[dst(other + FIN[q])], dma_engine_mask=0x00FF,
-                                  remote_sem=T.sem.arr2, srcs=srcs, dsts=[T.peer[:, :]], alu_op=1),
-                RemoteDMATransfer(dst_ids=[dst(base + FIN[q]), dst(base + FIN[q])], dma_engine_mask=0xFF00,
-                                  remote_sem=T.sem.arr2, srcs=srcs, dsts=[T.mine[:, :], pc(T.res, q)], alu_op=1)],
+                RemoteDMATransfer(dst_ids=[dst(other + FIN[s])], dma_engine_mask=0x00FF,
+                                  remote_sem=arr2[c], srcs=srcs, dsts=[pc(T.peer, c)], alu_op=1),
+                RemoteDMATransfer(dst_ids=[dst(base + FIN[s]), dst(base + FIN[s])], dma_engine_mask=0xFF00,
+                                  remote_sem=arr2[c], srcs=srcs, dsts=[pc(T.mine, c), pc(T.res, q)], alu_op=1)],
                 local_sem=T.sem.read2)
+    else:
+        s = FIN.index(k)
+        peers = [base + j for j in range(8) if j != k]
+        for c in range(2):
+            q = 4 * c + s
+            g.wait_ge(arr2[c], 24)
+            g.remote_dma_fused([RemoteDMATransfer(
+                dst_ids=[dst(d) for d in peers], dma_engine_mask=0xFFFF, remote_sem=arr3[c],
+                srcs=[pc(T.mine, c), pc(T.peer, c)], dsts=[pc(T.res, q) for d in peers], alu_op=1)],
+                local_sem=T.sem.read3)
+            g.dma_start(pc(T.res, q), pc(T.peer, c), accum_op=AluOpType.add).then_inc(acc[c], 16)
 
-    q = FIN.index(k)
-    g.wait_ge(T.sem.arr2, 24)
-    peers = [base + j for j in range(8) if j != k]
-    g.remote_dma_fused([RemoteDMATransfer(
-        dst_ids=[dst(c) for c in peers], dma_engine_mask=0xFFFF, remote_sem=arr3[q // 4],
-        srcs=[T.mine[:, :], T.peer[:, :]], dsts=[pc(T.res, q) for c in peers], alu_op=1)],
-        local_sem=T.sem.read3)
-    g.dma_start(pc(T.res, q), T.peer[:, :], accum_op=AluOpType.add).then_inc(T.sem.acc, 16)
-
-    if not gate:
-        g.wait_ge(T.sem.acc, 16)
-    g.wait_ge(T.sem.arr3a, 64 if gate else 48)
-    g.dma_start(T.y1[:, 0:C], T.res[:, 0:C]).then_inc(T.sem.stored, 16)
-    if gate:
-        g.wait_ge(T.sem.acc, 16)
-    g.wait_ge(T.sem.arr3b, 48 if gate else 64)
-    g.dma_start(T.y1[:, C:1024], T.res[:, C:1024]).then_inc(T.sem.stored, 16)
-    g.dma_start(T.y3[:, :], T.res[:, 1024:1280]).then_inc(T.sem.stored, 16)
-    g.dma_start(T.y2[:, :], T.res[:, 1280:1284]).then_inc(T.sem.stored, 16)
+    for c in range(2):
+        if not gate:
+            g.wait_ge(acc[c], 16)
+        g.wait_ge(arr3[c], 64 if gate else 48)
+        if c == 0:
+            g.dma_start(T.y1[:, 0:C], T.res[:, 0:C]).then_inc(T.sem.stored, 16)
+        else:
+            g.dma_start(T.y1[:, C:1024], T.res[:, C:1024]).then_inc(T.sem.stored, 16)
+            g.dma_start(T.y3[:, :], T.res[:, 1024:1280]).then_inc(T.sem.stored, 16)
+            g.dma_start(T.y2[:, :], T.res[:, 1280:1284]).then_inc(T.sem.stored, 16)
     g.wait_ge(T.sem.read1, n1)
     if gate:
         g.wait_ge(T.sem.read2, 32)
-    g.wait_ge(T.sem.read3, 16)
+    else:
+        g.wait_ge(T.sem.read3, 32)
     g.wait_ge(T.sem.stored, 64)

@@ -1,17 +1,17 @@
 from concourse.bass import RemoteDMATransfer, DstId
 from concourse.mybir import AluOpType
 
-W = 1288
+W = 1284
 C = 644
-P = 161
+PW = [161, 160]
 GATE = [2, 3, 6, 7]
 FIN = [0, 1, 4, 5]
 
 SCRATCH = {
     "buf": ("sbuf", [128, W], "float32"),
-    "land": ("sbuf", [128, 14 * P], "float32"),
-    "mine": ("sbuf", [128, 2 * P], "float32"),
-    "peer": ("sbuf", [128, 2 * P], "float32"),
+    "land": ("sbuf", [128, 7 * 321], "float32"),
+    "mine": ("sbuf", [128, 321], "float32"),
+    "peer": ("sbuf", [128, 321], "float32"),
     "res": ("sbuf", [128, W], "float32"),
 }
 SEMAPHORES = ["load0", "load1", "read1", "read2", "read3", "arr1a", "arr1b", "arr2a", "arr2b", "arr3a", "arr3b",
@@ -34,51 +34,50 @@ def rank_program(g, core, T, topo):
         rid, pid, se = topo.addr(c)
         return DstId(rid=rid, pnc=pid)
 
-    def pc(t, q):
-        return t[:, q * P:(q + 1) * P]
+    def pc(t, c, j, n):
+        a = c * n * PW[0] + j * PW[c]
+        return t[:, a:a + PW[c]]
 
     g.dma_start(T.buf[:, 0:C], T.x1[:, 0:C]).then_inc(T.sem.load0, 16)
     g.dma_start(T.buf[:, C:1024], T.x1[:, C:1024]).then_inc(T.sem.load1, 16)
     g.dma_start(T.buf[:, 1024:1280], T.x3[:, :]).then_inc(T.sem.load1, 16)
     g.dma_start(T.buf[:, 1280:1284], T.x2[:, :]).then_inc(T.sem.load1, 16)
-    g.dma_start(T.buf[:, 1284:1288], T.x2[:, :]).then_inc(T.sem.load1, 16)
 
     n1 = 0
     for c in range(2):
-        g.wait_ge([T.sem.load0, T.sem.load1][c], [16, 64][c])
+        g.wait_ge([T.sem.load0, T.sem.load1][c], [16, 48][c])
         trs = []
         for s, gk in enumerate(GATE):
             if gk == k:
                 continue
             slot = k if k < gk else k - 1
             trs.append(RemoteDMATransfer(dst_ids=[dst(base + gk)], dma_engine_mask=0xF << (4 * s), remote_sem=arr1[c],
-                                         src=pc(T.buf, 4 * c + s), dst=pc(T.land, 7 * c + slot)))
+                                         src=pc(T.buf, c, s, 4), dst=pc(T.land, c, slot, 7)))
         g.remote_dma_fused(trs, local_sem=T.sem.read1)
         n1 += 4 * len(trs)
 
     if gate:
         s = GATE.index(k)
         for c in range(2):
-            q = 4 * c + s
             g.wait_ge(arr1[c], 28)
-            srcs = [pc(T.buf, q)] + [pc(T.land, 7 * c + j) for j in range(7)]
+            srcs = [pc(T.buf, c, s, 4)] + [pc(T.land, c, j, 7) for j in range(7)]
             g.remote_dma_fused([
                 RemoteDMATransfer(dst_ids=[dst(other + FIN[s])], dma_engine_mask=0x00FF,
-                                  remote_sem=arr2[c], srcs=srcs, dsts=[pc(T.peer, c)], alu_op=1),
+                                  remote_sem=arr2[c], srcs=srcs, dsts=[pc(T.peer, c, 0, 1)], alu_op=1),
                 RemoteDMATransfer(dst_ids=[dst(base + FIN[s]), dst(base + FIN[s])], dma_engine_mask=0xFF00,
-                                  remote_sem=arr2[c], srcs=srcs, dsts=[pc(T.mine, c), pc(T.res, q)], alu_op=1)],
+                                  remote_sem=arr2[c], srcs=srcs, dsts=[pc(T.mine, c, 0, 1), pc(T.res, c, s, 4)],
+                                  alu_op=1)],
                 local_sem=T.sem.read2)
     else:
         s = FIN.index(k)
         peers = [base + j for j in range(8) if j != k]
         for c in range(2):
-            q = 4 * c + s
             g.wait_ge(arr2[c], 24)
             g.remote_dma_fused([RemoteDMATransfer(
                 dst_ids=[dst(d) for d in peers], dma_engine_mask=0xFFFF, remote_sem=arr3[c],
-                srcs=[pc(T.mine, c), pc(T.peer, c)], dsts=[pc(T.res, q) for d in peers], alu_op=1)],
+                srcs=[pc(T.mine, c, 0, 1), pc(T.peer, c, 0, 1)], dsts=[pc(T.res, c, s, 4) for d in peers], alu_op=1)],
                 local_sem=T.sem.read3)
-            g.dma_start(pc(T.res, q), pc(T.peer, c), accum_op=AluOpType.add).then_inc(acc[c], 16)
+            g.dma_start(pc(T.res, c, s, 4), pc(T.peer, c, 0, 1), accum_op=AluOpType.add).then_inc(acc[c], 16)
 
     for c in range(2):
         if not gate:

@@ -2,8 +2,8 @@ from concourse.bass import RemoteDMATransfer, DstId
 from concourse.mybir import AluOpType
 
 W = 1284
-C = 644
-PW = [161, 160]
+C = 768
+PW = [192, 129]
 GATE = [2, 3, 6, 7]
 FIN = [0, 1, 4, 5]
 

from concourse.bass import RemoteDMATransfer, DstId
from concourse.mybir import AluOpType

W = 1284
C = 768
PW = [192, 129]
GATE = [2, 3, 6, 7]
FIN = [0, 1, 4, 5]

SCRATCH = {
    "buf": ("sbuf", [128, W], "float32"),
    "land": ("sbuf", [128, 7 * 321], "float32"),
    "mine": ("sbuf", [128, 321], "float32"),
    "peer": ("sbuf", [128, 321], "float32"),
    "res": ("sbuf", [128, W], "float32"),
}
SEMAPHORES = ["load0", "load1", "read1", "read2", "read3", "arr1a", "arr1b", "arr2a", "arr2b", "arr3a", "arr3b",
              "acc0", "acc1", "stored"]


def rank_program(g, core, T, topo):
    if T.rank_of(core) is None:
        return
    base = 8 * topo.chip(core)
    other = 8 * (topo.chip(core) ^ 1)
    k = core - base
    gate = k in GATE
    arr1 = [T.sem.arr1a, T.sem.arr1b]
    arr2 = [T.sem.arr2a, T.sem.arr2b]
    arr3 = [T.sem.arr3a, T.sem.arr3b]
    acc = [T.sem.acc0, T.sem.acc1]

    def dst(c):
        rid, pid, se = topo.addr(c)
        return DstId(rid=rid, pnc=pid)

    def pc(t, c, j, n):
        a = c * n * PW[0] + j * PW[c]
        return t[:, a:a + PW[c]]

    g.dma_start(T.buf[:, 0:C], T.x1[:, 0:C]).then_inc(T.sem.load0, 16)
    g.dma_start(T.buf[:, C:1024], T.x1[:, C:1024]).then_inc(T.sem.load1, 16)
    g.dma_start(T.buf[:, 1024:1280], T.x3[:, :]).then_inc(T.sem.load1, 16)
    g.dma_start(T.buf[:, 1280:1284], T.x2[:, :]).then_inc(T.sem.load1, 16)

    n1 = 0
    for c in range(2):
        g.wait_ge([T.sem.load0, T.sem.load1][c], [16, 48][c])
        trs = []
        for s, gk in enumerate(GATE):
            if gk == k:
                continue
            slot = k if k < gk else k - 1
            trs.append(RemoteDMATransfer(dst_ids=[dst(base + gk)], dma_engine_mask=0xF << (4 * s), remote_sem=arr1[c],
                                         src=pc(T.buf, c, s, 4), dst=pc(T.land, c, slot, 7)))
        g.remote_dma_fused(trs, local_sem=T.sem.read1)
        n1 += 4 * len(trs)

    if gate:
        s = GATE.index(k)
        for c in range(2):
            g.wait_ge(arr1[c], 28)
            srcs = [pc(T.buf, c, s, 4)] + [pc(T.land, c, j, 7) for j in range(7)]
            g.remote_dma_fused([
                RemoteDMATransfer(dst_ids=[dst(other + FIN[s])], dma_engine_mask=0x00FF,
                                  remote_sem=arr2[c], srcs=srcs, dsts=[pc(T.peer, c, 0, 1)], alu_op=1),
                RemoteDMATransfer(dst_ids=[dst(base + FIN[s]), dst(base + FIN[s])], dma_engine_mask=0xFF00,
                                  remote_sem=arr2[c], srcs=srcs, dsts=[pc(T.mine, c, 0, 1), pc(T.res, c, s, 4)],
                                  alu_op=1)],
                local_sem=T.sem.read2)
    else:
        s = FIN.index(k)
        peers = [base + j for j in range(8) if j != k]
        for c in range(2):
            g.wait_ge(arr2[c], 24)
            g.remote_dma_fused([RemoteDMATransfer(
                dst_ids=[dst(d) for d in peers], dma_engine_mask=0xFFFF, remote_sem=arr3[c],
                srcs=[pc(T.mine, c, 0, 1), pc(T.peer, c, 0, 1)], dsts=[pc(T.res, c, s, 4) for d in peers], alu_op=1)],
                local_sem=T.sem.read3)
            g.dma_start(pc(T.res, c, s, 4), pc(T.peer, c, 0, 1), accum_op=AluOpType.add).then_inc(acc[c], 16)

    for c in range(2):
        if not gate:
            g.wait_ge(acc[c], 16)
        g.wait_ge(arr3[c], 64 if gate else 48)
        if c == 0:
            g.dma_start(T.y1[:, 0:C], T.res[:, 0:C]).then_inc(T.sem.stored, 16)
        else:
            g.dma_start(T.y1[:, C:1024], T.res[:, C:1024]).then_inc(T.sem.stored, 16)
            g.dma_start(T.y3[:, :], T.res[:, 1024:1280]).then_inc(T.sem.stored, 16)
            g.dma_start(T.y2[:, :], T.res[:, 1280:1284]).then_inc(T.sem.stored, 16)
    g.wait_ge(T.sem.read1, n1)
    if gate:
        g.wait_ge(T.sem.read2, 32)
    else:
        g.wait_ge(T.sem.read3, 32)
    g.wait_ge(T.sem.stored, 64)
